import numpy as np
import ml_dtypes

BF16 = ml_dtypes.bfloat16


def bf(x):
    return np.asarray(x, np.float32).astype(BF16)


def f32(x):
    return np.asarray(x, np.float32)


def f64(x):
    return np.asarray(x).astype(np.float64)


def striped(idx):
    return np.tile(idx.reshape(-1, 16).T, (8, 1))


S, K, N, E, Q, H, O = 256, 256, 256, 2, 128, 256, 128


def sigmoid(v):
    return 1.0 / (1.0 + np.exp(-v))


def setup_inputs():
    return {"table": bf(np.random.standard_normal((K, S))), "w": bf(np.random.standard_normal((E, K, H)) / np.sqrt(K)), "b": f32(0.5 * np.random.standard_normal((H, E))), "w2": bf(np.random.standard_normal((E, H, O)) / np.sqrt(H)), "c": f32(0.2 + 0.8 * np.random.random_sample((1, N))), "offs": striped(np.sort(np.random.permutation(S).reshape(E, Q), axis=1).reshape(-1))}


def reference(table, w, b, w2, c, offs):
    idx = offs[:16].T.reshape(-1)
    x = f64(table)[:, idx]
    ys = []
    for e in range(E):
        t = f64(w)[e].T @ x[:, e * Q : (e + 1) * Q] + f64(b)[:, e : e + 1]
        t = t * sigmoid(t)
        ys.append(f64(w2)[e].T @ t)
    return np.concatenate(ys, axis=1) * f64(c)

import concourse.mybir as mybir

P = 128
S, K, N, E, Q, H, O = 256, 256, 256, 2, 128, 256, 128
KB = K // P
HB = H // P
LIST_ROWS = 16

FLOPS = 2 * N * K * H + 2 * N * H * O

BF16, F32, U16 = mybir.dt.bfloat16, mybir.dt.float32, mybir.dt.uint16
SILU = mybir.ActivationFunctionType.Silu
MULT = mybir.AluOpType.mult


def tile_rows_ffn2_silu_kernel(tc, table, w, b, w2, c, offs, out):
    nc = tc.nc
    with (
        tc.tile_pool(name="held", bufs=1) as held,
        tc.psum_pool(name="psum", bufs=1) as psum,
    ):
        offsets = held.tile([P, N // LIST_ROWS], U16, name="offsets")
        tokens = held.tile([P, KB, S], BF16, name="tokens")
        w1_sb = [held.tile([P, KB, H], BF16, name=f"w1_{e}") for e in range(E)]
        w2_sb = held.tile([P, E, HB, O], BF16, name="w2_sb")
        bias = held.tile([P, HB, E], F32, name="bias")
        gains = held.tile([P, N], F32, name="gains")

        nc.sync.dma_start(tokens[:], table.rearrange("(p a) s -> p a s", a=KB))
        nc.scalar.dma_start(w1_sb[0][:], w[0].rearrange("(p a) i -> p a i", a=KB))
        nc.sync.dma_start(offsets[:], offs)
        nc.scalar.dma_start(bias[:], b.rearrange("(m p) e -> p m e", p=P))
        nc.sync.dma_start(w1_sb[1][:], w[1].rearrange("(p a) i -> p a i", a=KB))
        nc.sync.dma_start(w2_sb[:], w2.rearrange("e (m p) o -> p e m o", p=P))
        nc.sync.dma_start(gains[:], c[0].partition_broadcast(P))

        warm_in = held.tile([P, 1], F32, name="warm_in")
        warm_out = held.tile([P, 1], F32, name="warm_out")
        nc.vector.memset(warm_in[:], 0.0)
        nc.scalar.activation(warm_out[:], warm_in[:], SILU)

        hidden = {}
        for e in range(E):
            piece = offsets[:, e * Q // LIST_ROWS : (e + 1) * Q // LIST_ROWS]
            for m in range(HB):
                pre = psum.tile([P, Q], F32, name=f"pre_{e}_{m}")
                for a in range(KB):
                    nc.tensor.matmul(
                        pre[:],
                        w1_sb[e][:, a, m * P : (m + 1) * P],
                        tokens[:, a, :].indirect(piece),
                        start=(a == 0),
                        stop=(a == KB - 1),
                    )
                hidden[e, m] = held.tile([P, Q], BF16, name=f"hidden_{e}_{m}")
                nc.scalar.activation(hidden[e, m][:], pre[:], SILU, bias=bias[:, m, e : e + 1])

        for e in range(E):
            columns = slice(e * Q, (e + 1) * Q)
            y = psum.tile([O, Q], F32, name=f"y_{e}")
            for m in range(HB):
                nc.tensor.matmul(y[:], w2_sb[:, e, m, :], hidden[e, m][:], start=(m == 0), stop=(m == HB - 1))
            scaled = held.tile([O, Q], F32, name=f"scaled_{e}")
            nc.vector.tensor_tensor(scaled[:], y[:], gains[:, columns], MULT)
            store_queue = nc.sync if e == 0 else nc.scalar
            store_queue.dma_start(out[:, columns], scaled[:])
